import numpy as np
import ml_dtypes


def mxq(x, axis, fmt="e4m3"):
    dtype, down = {"e4m3": (ml_dtypes.float8_e4m3fn, 7), "e5m2": (ml_dtypes.float8_e5m2, 14)}[fmt]
    v = np.moveaxis(np.asarray(x, np.float32).astype(ml_dtypes.bfloat16).astype(np.float64), axis, -1)
    blocks = v.reshape(v.shape[:-1] + (-1, 32))
    amax = np.abs(blocks).max(-1, keepdims=True)
    byte = np.maximum(np.where(amax > 0, np.frexp(amax)[1] - 1 + 127, 0) - down, 1)
    scale = np.exp2(byte - 127.0)
    codes = (blocks / scale).astype(np.float32).astype(dtype).astype(np.float64)
    return np.moveaxis((codes * scale).reshape(v.shape), -1, axis)


WIDE = False


def mx_kscale(k):
    if not WIDE:
        return np.ones(k)
    levels = np.array([10, -10, 5, -5, 0])
    if k % 512:
        return np.exp2(np.random.permutation(np.resize(levels, k // 32))).repeat(32)
    a = np.empty((k // 512, 16))
    for p in range(k // 512):
        a[p, :8] = np.random.permutation(np.resize(levels, 8))
        for g in range(8):
            far = levels[np.abs(levels - a[p, g]) >= 10]
            a[p, g + 8] = far[np.random.randint(len(far))]
    return np.exp2(a.ravel()).repeat(32)


def f64(x):
    return np.asarray(x).astype(np.float64)


def striped8(idx):
    return np.concatenate([x.reshape(-1, 16).T for x in idx]).astype(np.uint16)


def runs(offs, k):
    lists = np.stack([offs[16 * r : 16 * r + 16].T.reshape(-1) for r in range(8)]).astype(np.int64)
    return lists[np.arange(k) % 512 // 64]


def pack_weight(w):
    k, n = w.shape
    w = f64(np.asarray(w, np.float32).astype(ml_dtypes.bfloat16)).reshape(k // 32, 32, n)
    amax = np.abs(w).max(1)
    byte = np.clip(np.where(amax > 0, np.frexp(amax)[1] - 1 + 127 - 7, 1), 1, 254)
    scaled = (w * np.exp2(127.0 - byte)[:, None, :]).reshape(k, n).astype(np.float32)
    words = np.ascontiguousarray(scaled.reshape(k // 512, 128, 4, n).transpose(0, 1, 3, 2)).astype(ml_dtypes.float8_e4m3fn).view(np.uint8)
    return words, np.ascontiguousarray(byte.astype(np.uint8).reshape(k // 512, 16, n))


def unpack_weight(words, scales):
    g, p, n, _ = words.shape
    vals = np.ascontiguousarray(words).view(ml_dtypes.float8_e4m3fn).astype(np.float64) * np.repeat(np.exp2(scales.astype(np.float64) - 127.0), 8, axis=1)[..., None]
    return vals.transpose(0, 1, 3, 2).reshape(g * 512, n)


def sigmoid(v):
    return 1.0 / (1.0 + np.exp(-np.maximum(v, -700.0)))

def planes(y):
    n, m = y.shape
    v = y.astype(np.float32).astype(ml_dtypes.bfloat16).astype(np.float64).reshape(n // 32, 32, m)
    top = np.abs(v).max(1)
    byte = np.clip(np.where(top > 0, np.frexp(top)[1] - 1 + 127 - 7, 1), 1, 254)
    codes = (v * np.exp2(127.0 - byte)[:, None, :]).reshape(n, m).astype(np.float32).astype(ml_dtypes.float8_e4m3fn).view(np.uint8)
    words = codes.reshape(n // 512, 128, 4, m).transpose(0, 1, 3, 2)
    return np.ascontiguousarray(words), np.ascontiguousarray(byte.astype(np.uint8).reshape(n // 512, 16, m))


K, T, S, N, H, W = 512, 2048, 512, 512, 512, 256


def setup_inputs():
    n = np.random.standard_normal
    s = mx_kscale(K)[:, None]
    u = mx_kscale(H)
    packed_xT = pack_weight(n((K, T)) * s)
    packed_w1 = pack_weight(n((K, H)) / np.sqrt(K) / s)
    packed_w2 = pack_weight(n((H, N)) / np.sqrt(H) / u[:, None])
    perm = np.stack([np.random.permutation(S) for _ in range(8)])
    return {
        "x_words": packed_xT[0],
        "x_scales": packed_xT[1],
        "w1_words": packed_w1[0],
        "w1_scales": packed_w1[1],
        "gn": (np.random.uniform(0.5, 1.5, (H, 1)) * u[:, None]).astype(np.float32),
        "w2_words": packed_w2[0],
        "w2_scales": packed_w2[1],
        "offs": striped8(np.random.randint(0, T, (8, S))),
        "n1": striped8(perm[:, :W]),
        "n2": striped8(perm[:, W:]),
        "n3": striped8(np.stack([np.random.permutation(S) for _ in range(8)])),
        "n4": striped8(np.stack([np.random.permutation(S) for _ in range(8)])),
    }


def reference(x_words, x_scales, w1_words, w1_scales, gn, w2_words, w2_scales, offs, n1, n2, n3, n4):
    xq = unpack_weight(x_words, x_scales)[np.arange(K)[:, None], runs(offs, K)]
    y = unpack_weight(w1_words, w1_scales).T @ xq
    pa = y[np.arange(H)[:, None], runs(n1, H)]
    pb = y[np.arange(H)[:, None], runs(n2, H)]
    rb = np.maximum(0.5 * pa, pb)
    ra = pb - pa
    ds = np.zeros((H, S))
    ds[np.arange(H)[:, None], runs(n1, H)] = ra
    dt = ds.copy()
    dt[np.arange(H)[:, None], runs(n2, H)] = rb
    z = f64(gn) * dt
    h = unpack_weight(w2_words, w2_scales).T @ mxq(z, 0, "e4m3")
    out_0 = h * (sigmoid(h[np.arange(N)[:, None], runs(n3, N)] - (h[np.arange(N)[:, None], runs(n4, N)])))
    return (out_0,) + planes(out_0)

@@ -1,0 +1,274 @@
+from contextlib import ExitStack
+
+import concourse.mybir as mybir
+
+K, T, S, N, H, W = 512, 2048, 512, 512, 512, 256
+FLOPS = 2 * K * H * S + 2 * H * N * S
+
+F32 = mybir.dt.float32
+BF16 = mybir.dt.bfloat16
+I32 = mybir.dt.int32
+U32 = mybir.dt.uint32
+U16 = mybir.dt.uint16
+U8 = mybir.dt.uint8
+FP8X4 = mybir.dt.float8_e4m3fn_x4
+ALU = mybir.AluOpType
+ACT = mybir.ActivationFunctionType
+
+P = 128
+PACK = 4
+HALF = S // 2
+PLANE_ORDER = (0, 2, 3, 1)
+CHUNKS = (256, 128, 128)
+
+
+def words_of(ap):
+    return ap[0].rearrange("p n t -> p (n t)").bitcast(I32)
+
+
+def load_scale_rows(engine, tile, scales, quadrants):
+    for q in quadrants:
+        engine.dma_start(out=tile[32 * q : 32 * q + 4, :].bitcast(I32), in_=scales[0, 4 * q : 4 * q + 4, :].bitcast(I32))
+
+
+def deal_words(nc, dealt, raw, planes):
+    nc.vector.tensor_copy(
+        out=dealt[:].rearrange("p (t a i) -> p a t i", t=PACK, i=4)[:, :, planes, :],
+        in_=raw[:].rearrange("p (a i t) -> p a t i", t=PACK, i=4)[:, :, planes, :],
+    )
+
+
+def deal_scales(nc, dealt, raw):
+    nc.vector.tensor_copy(
+        out=dealt[:].rearrange("p (t m) -> p t m", t=PACK),
+        in_=raw[:].rearrange("p (m t) -> p t m", t=PACK),
+    )
+
+
+def product(nc, bank, w_codes, w_scales, t, codes, scales):
+    rows = slice(P * t, P * (t + 1))
+    nc.tensor.matmul_mx(
+        out=bank,
+        lhsT=w_codes[:, rows].bitcast(FP8X4),
+        lhsT_scale=w_scales[:, rows],
+        rhs=codes.bitcast(FP8X4),
+        rhs_scale=scales,
+        start=True,
+        stop=True,
+    )
+
+
+def tile_picked_hashliftcmp_none_po_kernel(
+    tc, x_words, x_scales, w1_words, w1_scales, gn, w2_words, w2_scales, offs, n1, n2, n3, n4, out_0, out_1, out_2
+):
+    nc = tc.nc
+    with ExitStack() as ctx:
+        lists = ctx.enter_context(tc.tile_pool(name="lists", bufs=1))
+        keep = ctx.enter_context(tc.tile_pool(name="keep", bufs=1))
+        ring = ctx.enter_context(tc.tile_pool(name="ring", bufs=4))
+        psum = ctx.enter_context(tc.psum_pool(name="psum", bufs=1))
+
+        offs_sb = lists.tile([P, S // 16], U16, name="offs_sb")
+        n1_sb = lists.tile([P, W // 16], U16, name="n1_sb")
+        n2_sb = lists.tile([P, W // 16], U16, name="n2_sb")
+        n3_sb = lists.tile([P, S // 16], U16, name="n3_sb")
+        n4_sb = lists.tile([P, S // 16], U16, name="n4_sb")
+
+        x_tab = keep.tile([P, T], I32, name="x_tab", align_bytes=64)
+        xs_tab = keep.tile([P, T], U8, name="xs_tab", tag="xs_then_pick", align_bytes=64)
+        w1_raw = keep.tile([P, H], I32, name="w1_raw", align_bytes=64)
+        w1s_raw = keep.tile([P, H], U8, name="w1s_raw", align_bytes=64)
+        w2_raw = keep.tile([P, N], I32, name="w2_raw", align_bytes=64)
+        w2s_raw = keep.tile([P, N], U8, name="w2s_raw", align_bytes=64)
+        gain = keep.tile([P, PACK], F32, name="gain")
+        warm_in = keep.tile([P, 1], F32, name="warm_in")
+        warm_out = keep.tile([P, 1], F32, name="warm_out")
+
+        xs_got = keep.tile([P, S], U8, name="xs_got", align_bytes=64)
+        xs_pick = keep.tile([P, S], U8, name="xs_pick", align_bytes=64)
+
+        nc.vector.memset(xs_tab[:].bitcast(I32), 0)
+        nc.vector.memset(w1s_raw[:].bitcast(I32), 0)
+        nc.vector.memset(warm_in[:], 0.0)
+        nc.vector.memset(w2s_raw[:].bitcast(I32), 0)
+        nc.vector.memset(xs_pick[:].bitcast(I32), 0)
+
+        nc.sync.dma_start(offs_sb[:], offs)
+        nc.scalar.dma_start(out=xs_tab[0:P:8, :].bitcast(I32), in_=x_scales[0].bitcast(I32))
+        nc.gpsimd.dma_start(out=w1_raw[:], in_=words_of(w1_words))
+        nc.sync.dma_start(n1_sb[:], n1)
+        nc.sync.dma_start(n2_sb[:], n2)
+        nc.sync.dma_start(out=x_tab[:], in_=words_of(x_words))
+        load_scale_rows(nc.scalar, w1s_raw, w1_scales, range(4))
+        nc.scalar.activation(out=warm_out[:], in_=warm_in[:], func=ACT.Sigmoid)
+        nc.sync.dma_start(n3_sb[:], n3)
+        nc.sync.dma_start(n4_sb[:], n4)
+        load_scale_rows(nc.gpsimd, w2s_raw, w2_scales, range(2))
+        nc.gpsimd.dma_start(out=w2_raw[:], in_=words_of(w2_words))
+        load_scale_rows(nc.gpsimd, w2s_raw, w2_scales, range(2, 4))
+        nc.gpsimd.dma_start(out=gain[:], in_=gn.rearrange("(p t) o -> p (t o)", t=PACK))
+
+        nc.vector.tensor_copy(out=xs_got[:], in_=xs_tab[:].indirect(offs_sb[:]))
+        for j in range(4):
+            engine = nc.sync if j % 2 == 0 else nc.scalar
+            engine.dma_start(out=xs_pick[j:P:32, :].bitcast(I32), in_=xs_got[8 * j : P : 32, :].bitcast(I32))
+
+        w1_codes = keep.tile([P, H], I32, name="w1_codes", align_bytes=64)
+        w1_sc = keep.tile([P, H], U8, name="w1_sc", align_bytes=64)
+        deal_words(nc, w1_codes, w1_raw, slice(0, PACK))
+        deal_scales(nc, w1_sc, w1s_raw)
+
+        x_pick = keep.tile([P, S], I32, name="x_pick", tag="xs_then_pick", align_bytes=64)
+        halves = [slice(0, HALF), slice(HALF, S)]
+        for c in range(2):
+            nc.vector.tensor_copy(
+                out=x_pick[:, halves[c]].bitcast(U32),
+                in_=x_tab[:].bitcast(U32).indirect(offs_sb[:, c * HALF // 16 : (c + 1) * HALF // 16]),
+            )
+
+        w2_codes = keep.tile([P, N], I32, name="w2_codes", align_bytes=64)
+        w2_sc = keep.tile([P, N], U8, name="w2_sc", align_bytes=64)
+
+        def rows_out(name, w_codes, w_scales, codes, scales, order):
+            tiles = {}
+            for n, t in enumerate(order):
+                tile = keep.tile([P, S], F32, name="%s%d" % (name, t))
+                if n == 0:
+                    for c in range(2):
+                        bank = psum.tile([P, HALF], F32, name="%s_half%d" % (name, c), tag="half%d" % c)
+                        product(nc, bank[:], w_codes, w_scales, t, codes[:, halves[c]], scales[:, halves[c]])
+                        if c == 0:
+                            nc.scalar.copy(out=tile[:, halves[c]], in_=bank[:])
+                        else:
+                            nc.vector.tensor_copy(out=tile[:, halves[c]], in_=bank[:])
+                else:
+                    bank = psum.tile([P, S], F32, name="%s_bank%d" % (name, n), tag="bank%d" % n)
+                    product(nc, bank[:], w_codes, w_scales, t, codes[:], scales[:])
+                    nc.scalar.copy(out=tile[:], in_=bank[:])
+                tiles[t] = tile
+            return tiles
+
+        deal_words(nc, w2_codes, w2_raw, slice(0, PACK))
+        y = rows_out("y", w1_codes, w1_sc, x_pick, xs_pick, PLANE_ORDER)
+
+        z_bf = keep.tile([P, S, PACK], BF16, name="z_bf", align_bytes=64)
+        a, na, v, rv, dt = {}, {}, {}, {}, {}
+
+        def fetch_a(t):
+            a[t] = ring.tile([P, W], F32, name="a")
+            na[t] = ring.tile([P, W], F32, name="na")
+            nc.vector.tensor_scalar(
+                out=a[t][:], in0=y[t][:].indirect(n1_sb[:]), scalar1=0.5, scalar2=0.0, op0=ALU.mult, op1=ALU.add
+            )
+            nc.scalar.activation(out=na[t][:], in_=a[t][:], func=ACT.Copy, scale=-1.0)
+
+        def fetch_v(t):
+            v[t] = ring.tile([P, W], F32, name="v")
+            rv[t] = ring.tile([P, W], F32, name="rv")
+            nc.vector.tensor_tensor(out=v[t][:], in0=y[t][:].indirect(n2_sb[:]), in1=a[t][:], op=ALU.subtract)
+            nc.scalar.activation(out=rv[t][:], in_=v[t][:], func=ACT.Relu)
+
+        def put_ra(t):
+            dt[t] = ring.tile([P, S], F32, name="dt")
+            nc.vector.tensor_tensor(out=dt[t][:].indirect(n1_sb[:]), in0=v[t][:], in1=na[t][:], op=ALU.add)
+
+        def put_rb(t):
+            nc.vector.tensor_tensor(out=dt[t][:].indirect(n2_sb[:]), in0=a[t][:], in1=rv[t][:], op=ALU.add)
+
+        def scale_on_scalar(t, cols):
+            nc.scalar.activation(out=z_bf[:, cols, t], in_=dt[t][:, cols], func=ACT.Copy, scale=gain[:, t : t + 1])
+
+        def scale_on_vector(t, cols):
+            nc.vector.tensor_scalar(
+                out=z_bf[:, cols, t], in0=dt[t][:, cols], scalar1=gain[:, t : t + 1], scalar2=None, op0=ALU.mult
+            )
+
+        fetch_a(PLANE_ORDER[0])
+        deal_scales(nc, w2_sc, w2s_raw)
+        fetch_v(PLANE_ORDER[0])
+        for n, t in enumerate(PLANE_ORDER[:-1]):
+            fetch_a(PLANE_ORDER[n + 1])
+            put_ra(t)
+            fetch_v(PLANE_ORDER[n + 1])
+            put_rb(t)
+            scale_on_scalar(t, slice(0, S))
+        last = PLANE_ORDER[-1]
+        put_ra(last)
+        put_rb(last)
+        scale_on_scalar(last, slice(256, 384))
+        scale_on_vector(last, slice(0, 256))
+        scale_on_vector(last, slice(384, 512))
+
+        z_codes = keep.tile([P, S], I32, name="z_codes", align_bytes=64)
+        z_sc = keep.tile([P, S], U8, name="z_sc", align_bytes=64)
+        for c in range(2):
+            nc.vector.quantize_mx(
+                out=z_codes[:, halves[c]].bitcast(FP8X4),
+                scales=z_sc[:, halves[c]],
+                in_=z_bf[:, halves[c], :].rearrange("p j t -> p (j t)"),
+            )
+
+        h = rows_out("h", w2_codes, w2_sc, z_codes, z_sc, range(PACK))
+
+        o_codes = keep.tile([P, S], I32, name="o_codes", align_bytes=64)
+        o_sc = keep.tile([P, S], U8, name="o_sc", align_bytes=64)
+        out_rows = out_0.rearrange("(p t) j -> p t j", t=PACK)
+        out_words = words_of(out_1)
+
+        steps = []
+        start = 0
+        for width in CHUNKS:
+            steps.extend([(start, width, t) for t in range(PACK)])
+            start = start + width
+        first, gate, res = {}, {}, {}
+
+        def entries(sb, start, width):
+            return sb[:, start // 16 : (start + width) // 16]
+
+        def fetch_first(step):
+            start, width, t = step
+            first[step] = ring.tile([P, width], F32, name="first")
+            nc.vector.tensor_copy(out=first[step][:], in_=h[t][:].indirect(entries(n3_sb, start, width)))
+
+        def fetch_diff(step):
+            start, width, t = step
+            diff = ring.tile([P, width], F32, name="diff")
+            gate[step] = ring.tile([P, width], F32, name="gate")
+            nc.vector.tensor_tensor(
+                out=diff[:], in0=h[t][:].indirect(entries(n4_sb, start, width)), in1=first[step][:], op=ALU.subtract
+            )
+            nc.scalar.activation(out=gate[step][:], in_=diff[:], func=ACT.Sigmoid, scale=-1.0)
+
+        def finish(step):
+            start, width, t = step
+            cols = slice(start, start + width)
+            if t == 0:
+                res[start] = keep.tile([P, PACK, width], F32, name="res%d" % start)
+            nc.vector.tensor_tensor(out=res[start][:, t, :], in0=h[t][:, cols], in1=gate[step][:], op=ALU.mult)
+            if t == PACK - 1:
+                nc.sync.dma_start(out=out_rows[:, :, cols], in_=res[start][:])
+                o_bf = keep.tile([P, width, PACK], BF16, name="o_bf%d" % start, align_bytes=64)
+                dst = o_bf[:].rearrange("p (c i) t -> p c t i", i=4)
+                src = res[start][:].rearrange("p t (c i) -> p c t i", i=4)
+                if start + width < S:
+                    nc.scalar.copy(out=dst, in_=src)
+                else:
+                    nc.vector.tensor_copy(out=dst, in_=src)
+                nc.vector.quantize_mx(
+                    out=o_codes[:, cols].bitcast(FP8X4),
+                    scales=o_sc[:, cols],
+                    in_=o_bf[:].rearrange("p j t -> p (j t)"),
+                )
+                nc.sync.dma_start(out=out_words[:, cols], in_=o_codes[:, cols])
+
+        for n in range(len(steps) + 2):
+            if n < len(steps):
+                fetch_first(steps[n])
+            if 0 <= n - 2:
+                finish(steps[n - 2])
+            if 0 <= n - 1 < len(steps):
+                fetch_diff(steps[n - 1])
+
+        for q in range(4):
+            engine = nc.scalar if q % 2 == 0 else nc.sync
+            engine.dma_start(out=out_2[0, 4 * q : 4 * q + 4, :].bitcast(I32), in_=o_sc[32 * q : 32 * q + 4, :].bitcast(I32))

@@ -74,9 +74,9 @@ def tile_picked_hashliftcmp_none_po_kernel(
         n3_sb = lists.tile([P, S // 16], U16, name="n3_sb")
         n4_sb = lists.tile([P, S // 16], U16, name="n4_sb")
 
-        x_tab = keep.tile([P, T], I32, name="x_tab", align_bytes=64)
-        xs_tab = keep.tile([P, T], U8, name="xs_tab", tag="xs_then_pick", align_bytes=64)
-        w1_raw = keep.tile([P, H], I32, name="w1_raw", align_bytes=64)
+        x_tab = keep.tile([P, T], I32, name="x_tab", tag="x_then_w2", align_bytes=64)
+        xs_tab = keep.tile([P, T], U8, name="xs_tab", tag="xs_then_w1", align_bytes=64)
+        w1_raw = keep.tile([P, H], I32, name="w1_raw", tag="w1_then_pick", align_bytes=64)
         w1s_raw = keep.tile([P, H], U8, name="w1s_raw", align_bytes=64)
         w2_raw = keep.tile([P, N], I32, name="w2_raw", align_bytes=64)
         w2s_raw = keep.tile([P, N], U8, name="w2s_raw", align_bytes=64)
@@ -87,38 +87,42 @@ def tile_picked_hashliftcmp_none_po_kernel(
         xs_got = keep.tile([P, S], U8, name="xs_got", align_bytes=64)
         xs_pick = keep.tile([P, S], U8, name="xs_pick", align_bytes=64)
 
-        nc.vector.memset(xs_tab[:].bitcast(I32), 0)
-        nc.vector.memset(w1s_raw[:].bitcast(I32), 0)
         nc.vector.memset(warm_in[:], 0.0)
         nc.vector.memset(w2s_raw[:].bitcast(I32), 0)
         nc.vector.memset(xs_pick[:].bitcast(I32), 0)
 
         nc.sync.dma_start(offs_sb[:], offs)
-        nc.scalar.dma_start(out=xs_tab[0:P:8, :].bitcast(I32), in_=x_scales[0].bitcast(I32))
+        nc.scalar.dma_start(
+            out=xs_tab[:].bitcast(I32), in_=x_scales[0].bitcast(I32).unsqueeze(1).to_broadcast([16, 8, T // 4])
+        )
+        nc.scalar.dma_start(out=x_tab[:], in_=words_of(x_words))
         nc.gpsimd.dma_start(out=w1_raw[:], in_=words_of(w1_words))
+        for q in range(4):
+            nc.sync.dma_start(
+                out=w1s_raw[32 * q : 32 * q + 32, :].bitcast(I32),
+                in_=w1_scales[0, 4 * q : 4 * q + 4, :].bitcast(I32).unsqueeze(0).to_broadcast([8, 4, H // 4]),
+            )
+        nc.scalar.activation(out=warm_out[:], in_=warm_in[:], func=ACT.Sigmoid)
         nc.sync.dma_start(n1_sb[:], n1)
         nc.sync.dma_start(n2_sb[:], n2)
-        nc.sync.dma_start(out=x_tab[:], in_=words_of(x_words))
-        load_scale_rows(nc.scalar, w1s_raw, w1_scales, range(4))
-        nc.scalar.activation(out=warm_out[:], in_=warm_in[:], func=ACT.Sigmoid)
         nc.sync.dma_start(n3_sb[:], n3)
         nc.sync.dma_start(n4_sb[:], n4)
-        load_scale_rows(nc.gpsimd, w2s_raw, w2_scales, range(2))
+        nc.sync.dma_start(out=gain[:], in_=gn.rearrange("(p t) o -> p (t o)", t=PACK))
         nc.gpsimd.dma_start(out=w2_raw[:], in_=words_of(w2_words))
-        load_scale_rows(nc.gpsimd, w2s_raw, w2_scales, range(2, 4))
-        nc.gpsimd.dma_start(out=gain[:], in_=gn.rearrange("(p t) o -> p (t o)", t=PACK))
+        load_scale_rows(nc.gpsimd, w2s_raw, w2_scales, range(4))
 
         nc.vector.tensor_copy(out=xs_got[:], in_=xs_tab[:].indirect(offs_sb[:]))
-        for j in range(4):
-            engine = nc.sync if j % 2 == 0 else nc.scalar
-            engine.dma_start(out=xs_pick[j:P:32, :].bitcast(I32), in_=xs_got[8 * j : P : 32, :].bitcast(I32))
+        for q in range(4):
+            nc.scalar.dma_start(
+                out=xs_pick[32 * q : 32 * q + 4, :].bitcast(I32), in_=xs_got[32 * q : 32 * q + 32 : 8, :].bitcast(I32)
+            )
 
-        w1_codes = keep.tile([P, H], I32, name="w1_codes", align_bytes=64)
+        w1_codes = keep.tile([P, H], I32, name="w1_codes", tag="xs_then_w1", align_bytes=64)
         w1_sc = keep.tile([P, H], U8, name="w1_sc", align_bytes=64)
         deal_words(nc, w1_codes, w1_raw, slice(0, PACK))
         deal_scales(nc, w1_sc, w1s_raw)
 
-        x_pick = keep.tile([P, S], I32, name="x_pick", tag="xs_then_pick", align_bytes=64)
+        x_pick = keep.tile([P, S], I32, name="x_pick", tag="w1_then_pick", align_bytes=64)
         halves = [slice(0, HALF), slice(HALF, S)]
         for c in range(2):
             nc.vector.tensor_copy(
@@ -126,13 +130,12 @@ def tile_picked_hashliftcmp_none_po_kernel(
                 in_=x_tab[:].bitcast(U32).indirect(offs_sb[:, c * HALF // 16 : (c + 1) * HALF // 16]),
             )
 
-        w2_codes = keep.tile([P, N], I32, name="w2_codes", align_bytes=64)
-        w2_sc = keep.tile([P, N], U8, name="w2_sc", align_bytes=64)
+        w2_codes = keep.tile([P, N], I32, name="w2_codes", tag="x_then_w2", align_bytes=64)
 
         def rows_out(name, w_codes, w_scales, codes, scales, order):
             tiles = {}
             for n, t in enumerate(order):
-                tile = keep.tile([P, S], F32, name="%s%d" % (name, t))
+                tile = keep.tile([P, S], F32, name="%s%d" % (name, t), align_bytes=64)
                 if n == 0:
                     for c in range(2):
                         bank = psum.tile([P, HALF], F32, name="%s_half%d" % (name, c), tag="half%d" % c)
@@ -184,7 +187,6 @@ def tile_picked_hashliftcmp_none_po_kernel(
             )
 
         fetch_a(PLANE_ORDER[0])
-        deal_scales(nc, w2_sc, w2s_raw)
         fetch_v(PLANE_ORDER[0])
         for n, t in enumerate(PLANE_ORDER[:-1]):
             fetch_a(PLANE_ORDER[n + 1])
@@ -194,6 +196,8 @@ def tile_picked_hashliftcmp_none_po_kernel(
             scale_on_scalar(t, slice(0, S))
         last = PLANE_ORDER[-1]
         put_ra(last)
+        w2_sc = keep.tile([P, N], U8, name="w2_sc", tag="y%d" % last, align_bytes=64)
+        deal_scales(nc, w2_sc, w2s_raw)
         put_rb(last)
         scale_on_scalar(last, slice(256, 384))
         scale_on_vector(last, slice(0, 256))

@@ -20,6 +20,7 @@ PACK = 4
 HALF = S // 2
 PLANE_ORDER = (0, 2, 3, 1)
 CHUNKS = (256, 128, 128)
+ON_GPSIMD = 3
 
 
 def words_of(ap):
@@ -28,7 +29,10 @@ def words_of(ap):
 
 def load_scale_rows(engine, tile, scales, quadrants):
     for q in quadrants:
-        engine.dma_start(out=tile[32 * q : 32 * q + 4, :].bitcast(I32), in_=scales[0, 4 * q : 4 * q + 4, :].bitcast(I32))
+        rows = scales[0, 4 * q : 4 * q + 4, :].bitcast(I32)
+        engine.dma_start(
+            out=tile[32 * q : 32 * q + 32, :].bitcast(I32), in_=rows.unsqueeze(0).to_broadcast([8, 4, rows.shape[1]])
+        )
 
 
 def deal_words(nc, dealt, raw, planes):
@@ -65,7 +69,7 @@ def tile_picked_hashliftcmp_none_po_kernel(
     with ExitStack() as ctx:
         lists = ctx.enter_context(tc.tile_pool(name="lists", bufs=1))
         keep = ctx.enter_context(tc.tile_pool(name="keep", bufs=1))
-        ring = ctx.enter_context(tc.tile_pool(name="ring", bufs=4))
+        ring = ctx.enter_context(tc.tile_pool(name="ring", bufs=6))
         psum = ctx.enter_context(tc.psum_pool(name="psum", bufs=1))
 
         offs_sb = lists.tile([P, S // 16], U16, name="offs_sb")
@@ -74,9 +78,9 @@ def tile_picked_hashliftcmp_none_po_kernel(
         n3_sb = lists.tile([P, S // 16], U16, name="n3_sb")
         n4_sb = lists.tile([P, S // 16], U16, name="n4_sb")
 
-        x_tab = keep.tile([P, T], I32, name="x_tab", tag="x_then_w2", align_bytes=64)
-        xs_tab = keep.tile([P, T], U8, name="xs_tab", tag="xs_then_w1", align_bytes=64)
-        w1_raw = keep.tile([P, H], I32, name="w1_raw", tag="w1_then_pick", align_bytes=64)
+        x_tab = keep.tile([P, T], I32, name="x_tab", tag="x_then_w1", align_bytes=64)
+        xs_tab = keep.tile([P, T], U8, name="xs_tab", tag="xs_then_w1s", align_bytes=64)
+        w1_raw = keep.tile([P, H], I32, name="w1_raw", tag="w1_then_w2", align_bytes=64)
         w1s_raw = keep.tile([P, H], U8, name="w1s_raw", align_bytes=64)
         w2_raw = keep.tile([P, N], I32, name="w2_raw", align_bytes=64)
         w2s_raw = keep.tile([P, N], U8, name="w2s_raw", align_bytes=64)
@@ -88,7 +92,6 @@ def tile_picked_hashliftcmp_none_po_kernel(
         xs_pick = keep.tile([P, S], U8, name="xs_pick", align_bytes=64)
 
         nc.vector.memset(warm_in[:], 0.0)
-        nc.vector.memset(w2s_raw[:].bitcast(I32), 0)
         nc.vector.memset(xs_pick[:].bitcast(I32), 0)
 
         nc.sync.dma_start(offs_sb[:], offs)
@@ -97,19 +100,16 @@ def tile_picked_hashliftcmp_none_po_kernel(
         )
         nc.scalar.dma_start(out=x_tab[:], in_=words_of(x_words))
         nc.gpsimd.dma_start(out=w1_raw[:], in_=words_of(w1_words))
-        for q in range(4):
-            nc.sync.dma_start(
-                out=w1s_raw[32 * q : 32 * q + 32, :].bitcast(I32),
-                in_=w1_scales[0, 4 * q : 4 * q + 4, :].bitcast(I32).unsqueeze(0).to_broadcast([8, 4, H // 4]),
-            )
+        load_scale_rows(nc.sync, w1s_raw, w1_scales, range(4))
         nc.scalar.activation(out=warm_out[:], in_=warm_in[:], func=ACT.Sigmoid)
         nc.sync.dma_start(n1_sb[:], n1)
         nc.sync.dma_start(n2_sb[:], n2)
         nc.sync.dma_start(n3_sb[:], n3)
         nc.sync.dma_start(n4_sb[:], n4)
         nc.sync.dma_start(out=gain[:], in_=gn.rearrange("(p t) o -> p (t o)", t=PACK))
+        load_scale_rows(nc.gpsimd, w2s_raw, w2_scales, range(1))
         nc.gpsimd.dma_start(out=w2_raw[:], in_=words_of(w2_words))
-        load_scale_rows(nc.gpsimd, w2s_raw, w2_scales, range(4))
+        load_scale_rows(nc.gpsimd, w2s_raw, w2_scales, range(1, 4))
 
         nc.vector.tensor_copy(out=xs_got[:], in_=xs_tab[:].indirect(offs_sb[:]))
         for q in range(4):
@@ -117,12 +117,10 @@ def tile_picked_hashliftcmp_none_po_kernel(
                 out=xs_pick[32 * q : 32 * q + 4, :].bitcast(I32), in_=xs_got[32 * q : 32 * q + 32 : 8, :].bitcast(I32)
             )
 
-        w1_codes = keep.tile([P, H], I32, name="w1_codes", tag="xs_then_w1", align_bytes=64)
-        w1_sc = keep.tile([P, H], U8, name="w1_sc", align_bytes=64)
-        deal_words(nc, w1_codes, w1_raw, slice(0, PACK))
+        w1_sc = keep.tile([P, H], U8, name="w1_sc", tag="xs_then_w1s", align_bytes=64)
         deal_scales(nc, w1_sc, w1s_raw)
 
-        x_pick = keep.tile([P, S], I32, name="x_pick", tag="w1_then_pick", align_bytes=64)
+        x_pick = keep.tile([P, S], I32, name="x_pick", align_bytes=64)
         halves = [slice(0, HALF), slice(HALF, S)]
         for c in range(2):
             nc.vector.tensor_copy(
@@ -130,29 +128,26 @@ def tile_picked_hashliftcmp_none_po_kernel(
                 in_=x_tab[:].bitcast(U32).indirect(offs_sb[:, c * HALF // 16 : (c + 1) * HALF // 16]),
             )
 
-        w2_codes = keep.tile([P, N], I32, name="w2_codes", tag="x_then_w2", align_bytes=64)
+        w1_codes = keep.tile([P, H], I32, name="w1_codes", tag="x_then_w1", align_bytes=64)
+        deal_words(nc, w1_codes, w1_raw, slice(0, 1))
+        deal_words(nc, w1_codes, w1_raw, slice(1, PACK))
+        w2_codes = keep.tile([P, N], I32, name="w2_codes", tag="w1_then_w2", align_bytes=64)
 
-        def rows_out(name, w_codes, w_scales, codes, scales, order):
-            tiles = {}
+        def rows_out(name, w_codes, w_scales, codes, scales, order, pieces):
+            tiles, banks = {}, {}
             for n, t in enumerate(order):
                 tile = keep.tile([P, S], F32, name="%s%d" % (name, t), align_bytes=64)
-                if n == 0:
-                    for c in range(2):
-                        bank = psum.tile([P, HALF], F32, name="%s_half%d" % (name, c), tag="half%d" % c)
-                        product(nc, bank[:], w_codes, w_scales, t, codes[:, halves[c]], scales[:, halves[c]])
-                        if c == 0:
-                            nc.scalar.copy(out=tile[:, halves[c]], in_=bank[:])
-                        else:
-                            nc.vector.tensor_copy(out=tile[:, halves[c]], in_=bank[:])
-                else:
-                    bank = psum.tile([P, S], F32, name="%s_bank%d" % (name, n), tag="bank%d" % n)
-                    product(nc, bank[:], w_codes, w_scales, t, codes[:], scales[:])
-                    nc.scalar.copy(out=tile[:], in_=bank[:])
+                for c, cols in enumerate(pieces if n == 0 else [slice(0, S)]):
+                    tag = "piece%d" % c if n == 0 else "bank%d" % n
+                    bank = psum.tile([P, cols.stop - cols.start], F32, name="%s_%s" % (name, tag), tag=tag)
+                    product(nc, bank[:], w_codes, w_scales, t, codes[:, cols], scales[:, cols])
+                    nc.scalar.copy(out=tile[:, cols], in_=bank[:])
                 tiles[t] = tile
-            return tiles
+                banks[t] = bank
+            return tiles, banks
 
         deal_words(nc, w2_codes, w2_raw, slice(0, PACK))
-        y = rows_out("y", w1_codes, w1_sc, x_pick, xs_pick, PLANE_ORDER)
+        y, y_banks = rows_out("y", w1_codes, w1_sc, x_pick, xs_pick, PLANE_ORDER, halves)
 
         z_bf = keep.tile([P, S, PACK], BF16, name="z_bf", align_bytes=64)
         a, na, v, rv, dt = {}, {}, {}, {}, {}
@@ -199,20 +194,26 @@ def tile_picked_hashliftcmp_none_po_kernel(
         w2_sc = keep.tile([P, N], U8, name="w2_sc", tag="y%d" % last, align_bytes=64)
         deal_scales(nc, w2_sc, w2s_raw)
         put_rb(last)
-        scale_on_scalar(last, slice(256, 384))
-        scale_on_vector(last, slice(0, 256))
-        scale_on_vector(last, slice(384, 512))
-
+        quarters = [slice(c * P, (c + 1) * P) for c in range(4)]
         z_codes = keep.tile([P, S], I32, name="z_codes", align_bytes=64)
         z_sc = keep.tile([P, S], U8, name="z_sc", align_bytes=64)
-        for c in range(2):
+
+        def quantize_z(cols):
             nc.vector.quantize_mx(
-                out=z_codes[:, halves[c]].bitcast(FP8X4),
-                scales=z_sc[:, halves[c]],
-                in_=z_bf[:, halves[c], :].rearrange("p j t -> p (j t)"),
+                out=z_codes[:, cols].bitcast(FP8X4),
+                scales=z_sc[:, cols],
+                in_=z_bf[:, cols, :].rearrange("p j t -> p (j t)"),
             )
 
-        h = rows_out("h", w2_codes, w2_sc, z_codes, z_sc, range(PACK))
+        scale_on_scalar(last, quarters[3])
+        scale_on_vector(last, quarters[0])
+        scale_on_vector(last, quarters[1])
+        quantize_z(quarters[0])
+        scale_on_vector(last, quarters[2])
+        for cols in quarters[1:]:
+            quantize_z(cols)
+
+        h, h_banks = rows_out("h", w2_codes, w2_sc, z_codes, z_sc, range(PACK), quarters)
 
         o_codes = keep.tile([P, S], I32, name="o_codes", align_bytes=64)
         o_sc = keep.tile([P, S], U8, name="o_sc", align_bytes=64)
@@ -234,13 +235,17 @@ def tile_picked_hashliftcmp_none_po_kernel(
             first[step] = ring.tile([P, width], F32, name="first")
             nc.vector.tensor_copy(out=first[step][:], in_=h[t][:].indirect(entries(n3_sb, start, width)))
 
-        def fetch_diff(step):
+        def fetch_second(step):
             start, width, t = step
             diff = ring.tile([P, width], F32, name="diff")
             gate[step] = ring.tile([P, width], F32, name="gate")
-            nc.vector.tensor_tensor(
-                out=diff[:], in0=h[t][:].indirect(entries(n4_sb, start, width)), in1=first[step][:], op=ALU.subtract
-            )
+            looked_up = h[t][:].indirect(entries(n4_sb, start, width))
+            if start + width == S:
+                nc.vector.tensor_tensor(out=diff[:], in0=looked_up, in1=first[step][:], op=ALU.subtract)
+            else:
+                second = ring.tile([P, width], F32, name="second")
+                nc.vector.tensor_copy(out=second[:], in_=looked_up)
+                nc.gpsimd.tensor_tensor(out=diff[:], in0=second[:], in1=first[step][:], op=ALU.subtract)
             nc.scalar.activation(out=gate[step][:], in_=diff[:], func=ACT.Sigmoid, scale=-1.0)
 
         def finish(step):
@@ -248,31 +253,43 @@ def tile_picked_hashliftcmp_none_po_kernel(
             cols = slice(start, start + width)
             if t == 0:
                 res[start] = keep.tile([P, PACK, width], F32, name="res%d" % start)
-            nc.vector.tensor_tensor(out=res[start][:, t, :], in0=h[t][:, cols], in1=gate[step][:], op=ALU.mult)
+            parts = [slice(0, width // 2), slice(width // 2, width)] if step == steps[-1] else [slice(0, width)]
+            for part in parts:
+                at = slice(start + part.start, start + part.stop)
+                if t < ON_GPSIMD and start + width < S:
+                    nc.gpsimd.tensor_tensor(out=res[start][:, t, part], in0=h[t][:, at], in1=gate[step][:, part], op=ALU.mult)
+                else:
+                    nc.vector.tensor_tensor(
+                        out=res[start][:, t, part], in0=(h_banks[t] if t > 0 else h[t])[:, at], in1=gate[step][:, part], op=ALU.mult
+                    )
             if t == PACK - 1:
                 nc.sync.dma_start(out=out_rows[:, :, cols], in_=res[start][:])
                 o_bf = keep.tile([P, width, PACK], BF16, name="o_bf%d" % start, align_bytes=64)
-                dst = o_bf[:].rearrange("p (c i) t -> p c t i", i=4)
-                src = res[start][:].rearrange("p t (c i) -> p c t i", i=4)
-                if start + width < S:
-                    nc.scalar.copy(out=dst, in_=src)
-                else:
-                    nc.vector.tensor_copy(out=dst, in_=src)
-                nc.vector.quantize_mx(
-                    out=o_codes[:, cols].bitcast(FP8X4),
-                    scales=o_sc[:, cols],
-                    in_=o_bf[:].rearrange("p j t -> p (j t)"),
-                )
+                for part in parts:
+                    dst = o_bf[:, part, :].rearrange("p (c i) t -> p c t i", i=4)
+                    src = res[start][:, :, part].rearrange("p t (c i) -> p c t i", i=4)
+                    if step == steps[-1]:
+                        nc.vector.tensor_copy(out=dst, in_=src)
+                    else:
+                        nc.scalar.copy(out=dst, in_=src)
+                for part in parts:
+                    at = slice(start + part.start, start + part.stop)
+                    nc.vector.quantize_mx(
+                        out=o_codes[:, at].bitcast(FP8X4),
+                        scales=o_sc[:, at],
+                        in_=o_bf[:, part, :].rearrange("p j t -> p (j t)"),
+                    )
                 nc.sync.dma_start(out=out_words[:, cols], in_=o_codes[:, cols])
 
+        fetch_first(steps[0])
         for n in range(len(steps) + 2):
+            if n + 1 < len(steps):
+                fetch_first(steps[n + 1])
             if n < len(steps):
-                fetch_first(steps[n])
-            if 0 <= n - 2:
+                fetch_second(steps[n])
+            if n >= 2:
                 finish(steps[n - 2])
-            if 0 <= n - 1 < len(steps):
-                fetch_diff(steps[n - 1])
 
         for q in range(4):
-            engine = nc.scalar if q % 2 == 0 else nc.sync
+            engine = nc.scalar if q < 3 else nc.sync
             engine.dma_start(out=out_2[0, 4 * q : 4 * q + 4, :].bitcast(I32), in_=o_sc[32 * q : 32 * q + 4, :].bitcast(I32))

@@ -122,6 +122,7 @@ def tile_picked_hashliftcmp_none_po_kernel(
 
         x_pick = keep.tile([P, S], I32, name="x_pick", align_bytes=64)
         halves = [slice(0, HALF), slice(HALF, S)]
+        quarters = [slice(c * P, (c + 1) * P) for c in range(4)]
         for c in range(2):
             nc.vector.tensor_copy(
                 out=x_pick[:, halves[c]].bitcast(U32),
@@ -147,31 +148,43 @@ def tile_picked_hashliftcmp_none_po_kernel(
             return tiles, banks
 
         deal_words(nc, w2_codes, w2_raw, slice(0, PACK))
-        y, y_banks = rows_out("y", w1_codes, w1_sc, x_pick, xs_pick, PLANE_ORDER, halves)
+        y, y_banks = rows_out("y", w1_codes, w1_sc, x_pick, xs_pick, PLANE_ORDER, [halves[0]] + quarters[2:])
 
         z_bf = keep.tile([P, S, PACK], BF16, name="z_bf", align_bytes=64)
-        a, na, v, rv, dt = {}, {}, {}, {}, {}
+        a = keep.tile([P, PACK, W], F32, name="a")
+        na = keep.tile([P, PACK, W], F32, name="na")
+        v, rv, dt = {}, {}, {}
 
-        def fetch_a(t):
-            a[t] = ring.tile([P, W], F32, name="a")
-            na[t] = ring.tile([P, W], F32, name="na")
+        def fetch_a(n):
             nc.vector.tensor_scalar(
-                out=a[t][:], in0=y[t][:].indirect(n1_sb[:]), scalar1=0.5, scalar2=0.0, op0=ALU.mult, op1=ALU.add
+                out=a[:, n, :],
+                in0=y[PLANE_ORDER[n]][:].indirect(n1_sb[:]),
+                scalar1=0.5,
+                scalar2=0.0,
+                op0=ALU.mult,
+                op1=ALU.add,
             )
-            nc.scalar.activation(out=na[t][:], in_=a[t][:], func=ACT.Copy, scale=-1.0)
+            if n % 2 == 1:
+                nc.scalar.activation(out=na[:, n - 1 : n + 1, :], in_=a[:, n - 1 : n + 1, :], func=ACT.Copy, scale=-1.0)
 
-        def fetch_v(t):
-            v[t] = ring.tile([P, W], F32, name="v")
-            rv[t] = ring.tile([P, W], F32, name="rv")
-            nc.vector.tensor_tensor(out=v[t][:], in0=y[t][:].indirect(n2_sb[:]), in1=a[t][:], op=ALU.subtract)
-            nc.scalar.activation(out=rv[t][:], in_=v[t][:], func=ACT.Relu)
+        def fetch_v(n):
+            v[n] = ring.tile([P, W], F32, name="v")
+            nc.vector.tensor_tensor(
+                out=v[n][:], in0=y[PLANE_ORDER[n]][:].indirect(n2_sb[:]), in1=na[:, n, :], op=ALU.add
+            )
 
-        def put_ra(t):
-            dt[t] = ring.tile([P, S], F32, name="dt")
-            nc.vector.tensor_tensor(out=dt[t][:].indirect(n1_sb[:]), in0=v[t][:], in1=na[t][:], op=ALU.add)
+        def positive_part(n):
+            rv[n] = ring.tile([P, W], F32, name="rv")
+            nc.scalar.activation(out=rv[n][:], in_=v[n][:], func=ACT.Relu)
 
-        def put_rb(t):
-            nc.vector.tensor_tensor(out=dt[t][:].indirect(n2_sb[:]), in0=a[t][:], in1=rv[t][:], op=ALU.add)
+        def put_ra(n):
+            t = PLANE_ORDER[n]
+            dt[t] = keep.tile([P, S], F32, name="dt%d" % t, align_bytes=64)
+            nc.vector.tensor_tensor(out=dt[t][:].indirect(n1_sb[:]), in0=v[n][:], in1=na[:, n, :], op=ALU.add)
+
+        def put_rb(n):
+            t = PLANE_ORDER[n]
+            nc.vector.tensor_tensor(out=dt[t][:].indirect(n2_sb[:]), in0=a[:, n, :], in1=rv[n][:], op=ALU.add)
 
         def scale_on_scalar(t, cols):
             nc.scalar.activation(out=z_bf[:, cols, t], in_=dt[t][:, cols], func=ACT.Copy, scale=gain[:, t : t + 1])
@@ -181,20 +194,20 @@ def tile_picked_hashliftcmp_none_po_kernel(
                 out=z_bf[:, cols, t], in0=dt[t][:, cols], scalar1=gain[:, t : t + 1], scalar2=None, op0=ALU.mult
             )
 
-        fetch_a(PLANE_ORDER[0])
-        fetch_v(PLANE_ORDER[0])
-        for n, t in enumerate(PLANE_ORDER[:-1]):
-            fetch_a(PLANE_ORDER[n + 1])
-            put_ra(t)
-            fetch_v(PLANE_ORDER[n + 1])
-            put_rb(t)
-            scale_on_scalar(t, slice(0, S))
+        for n in range(PACK):
+            fetch_a(n)
+        for n in range(PACK):
+            fetch_v(n)
+            positive_part(n)
+        put_ra(0)
+        for n in range(PACK - 1):
+            put_ra(n + 1)
+            put_rb(n)
+            scale_on_scalar(PLANE_ORDER[n], slice(0, S))
         last = PLANE_ORDER[-1]
-        put_ra(last)
-        w2_sc = keep.tile([P, N], U8, name="w2_sc", tag="y%d" % last, align_bytes=64)
+        w2_sc = keep.tile([P, N], U8, name="w2_sc", tag="dt%d" % PLANE_ORDER[0], align_bytes=64)
         deal_scales(nc, w2_sc, w2s_raw)
-        put_rb(last)
-        quarters = [slice(c * P, (c + 1) * P) for c in range(4)]
+        put_rb(PACK - 1)
         z_codes = keep.tile([P, S], I32, name="z_codes", align_bytes=64)
         z_sc = keep.tile([P, S], U8, name="z_sc", align_bytes=64)
 
@@ -281,9 +294,11 @@ def tile_picked_hashliftcmp_none_po_kernel(
                     )
                 nc.sync.dma_start(out=out_words[:, cols], in_=o_codes[:, cols])
 
-        fetch_first(steps[0])
+        ahead = len(steps) - PACK
         for n in range(len(steps) + 2):
-            if n + 1 < len(steps):
+            if n <= ahead:
+                fetch_first(steps[n])
+            if ahead <= n < len(steps) - 1:
                 fetch_first(steps[n + 1])
             if n < len(steps):
                 fetch_second(steps[n])

@@ -143,8 +143,8 @@ def tile_picked_hashliftcmp_none_po_kernel(
                     bank = psum.tile([P, cols.stop - cols.start], F32, name="%s_%s" % (name, tag), tag=tag)
                     product(nc, bank[:], w_codes, w_scales, t, codes[:, cols], scales[:, cols])
                     nc.scalar.copy(out=tile[:, cols], in_=bank[:])
+                    banks[t, cols.start] = bank
                 tiles[t] = tile
-                banks[t] = bank
             return tiles, banks
 
         deal_words(nc, w2_codes, w2_raw, slice(0, PACK))
@@ -269,11 +269,11 @@ def tile_picked_hashliftcmp_none_po_kernel(
             parts = [slice(0, width // 2), slice(width // 2, width)] if step == steps[-1] else [slice(0, width)]
             for part in parts:
                 at = slice(start + part.start, start + part.stop)
-                if t < ON_GPSIMD and start + width < S:
+                if t < ON_GPSIMD and start == 0:
                     nc.gpsimd.tensor_tensor(out=res[start][:, t, part], in0=h[t][:, at], in1=gate[step][:, part], op=ALU.mult)
                 else:
                     nc.vector.tensor_tensor(
-                        out=res[start][:, t, part], in0=(h_banks[t] if t > 0 else h[t])[:, at], in1=gate[step][:, part], op=ALU.mult
+                        out=res[start][:, t, part], in0=h_banks[t, 0][:, at] if t > 0 else h_banks[t, start][:, part], in1=gate[step][:, part], op=ALU.mult
                     )
             if t == PACK - 1:
                 nc.sync.dma_start(out=out_rows[:, :, cols], in_=res[start][:])

from contextlib import ExitStack

import concourse.mybir as mybir

K, T, S, N, H, W = 512, 2048, 512, 512, 512, 256
FLOPS = 2 * K * H * S + 2 * H * N * S

F32 = mybir.dt.float32
BF16 = mybir.dt.bfloat16
I32 = mybir.dt.int32
U32 = mybir.dt.uint32
U16 = mybir.dt.uint16
U8 = mybir.dt.uint8
FP8X4 = mybir.dt.float8_e4m3fn_x4
ALU = mybir.AluOpType
ACT = mybir.ActivationFunctionType

P = 128
PACK = 4
HALF = S // 2
PLANE_ORDER = (0, 2, 3, 1)
CHUNKS = (256, 128, 128)
ON_GPSIMD = 3


def words_of(ap):
    return ap[0].rearrange("p n t -> p (n t)").bitcast(I32)


def load_scale_rows(engine, tile, scales, quadrants):
    for q in quadrants:
        rows = scales[0, 4 * q : 4 * q + 4, :].bitcast(I32)
        engine.dma_start(
            out=tile[32 * q : 32 * q + 32, :].bitcast(I32), in_=rows.unsqueeze(0).to_broadcast([8, 4, rows.shape[1]])
        )


def deal_words(nc, dealt, raw, planes):
    nc.vector.tensor_copy(
        out=dealt[:].rearrange("p (t a i) -> p a t i", t=PACK, i=4)[:, :, planes, :],
        in_=raw[:].rearrange("p (a i t) -> p a t i", t=PACK, i=4)[:, :, planes, :],
    )


def deal_scales(nc, dealt, raw):
    nc.vector.tensor_copy(
        out=dealt[:].rearrange("p (t m) -> p t m", t=PACK),
        in_=raw[:].rearrange("p (m t) -> p t m", t=PACK),
    )


def product(nc, bank, w_codes, w_scales, t, codes, scales):
    rows = slice(P * t, P * (t + 1))
    nc.tensor.matmul_mx(
        out=bank,
        lhsT=w_codes[:, rows].bitcast(FP8X4),
        lhsT_scale=w_scales[:, rows],
        rhs=codes.bitcast(FP8X4),
        rhs_scale=scales,
        start=True,
        stop=True,
    )


def tile_picked_hashliftcmp_none_po_kernel(
    tc, x_words, x_scales, w1_words, w1_scales, gn, w2_words, w2_scales, offs, n1, n2, n3, n4, out_0, out_1, out_2
):
    nc = tc.nc
    with ExitStack() as ctx:
        lists = ctx.enter_context(tc.tile_pool(name="lists", bufs=1))
        keep = ctx.enter_context(tc.tile_pool(name="keep", bufs=1))
        ring = ctx.enter_context(tc.tile_pool(name="ring", bufs=6))
        psum = ctx.enter_context(tc.psum_pool(name="psum", bufs=1))

        offs_sb = lists.tile([P, S // 16], U16, name="offs_sb")
        n1_sb = lists.tile([P, W // 16], U16, name="n1_sb")
        n2_sb = lists.tile([P, W // 16], U16, name="n2_sb")
        n3_sb = lists.tile([P, S // 16], U16, name="n3_sb")
        n4_sb = lists.tile([P, S // 16], U16, name="n4_sb")

        x_tab = keep.tile([P, T], I32, name="x_tab", tag="x_then_w1", align_bytes=64)
        xs_tab = keep.tile([P, T], U8, name="xs_tab", tag="xs_then_w1s", align_bytes=64)
        w1_raw = keep.tile([P, H], I32, name="w1_raw", tag="w1_then_w2", align_bytes=64)
        w1s_raw = keep.tile([P, H], U8, name="w1s_raw", align_bytes=64)
        w2_raw = keep.tile([P, N], I32, name="w2_raw", align_bytes=64)
        w2s_raw = keep.tile([P, N], U8, name="w2s_raw", align_bytes=64)
        gain = keep.tile([P, PACK], F32, name="gain")
        warm_in = keep.tile([P, 1], F32, name="warm_in")
        warm_out = keep.tile([P, 1], F32, name="warm_out")

        xs_got = keep.tile([P, S], U8, name="xs_got", align_bytes=64)
        xs_pick = keep.tile([P, S], U8, name="xs_pick", align_bytes=64)

        nc.vector.memset(warm_in[:], 0.0)
        nc.vector.memset(xs_pick[:].bitcast(I32), 0)

        nc.sync.dma_start(offs_sb[:], offs)
        nc.scalar.dma_start(
            out=xs_tab[:].bitcast(I32), in_=x_scales[0].bitcast(I32).unsqueeze(1).to_broadcast([16, 8, T // 4])
        )
        nc.scalar.dma_start(out=x_tab[:], in_=words_of(x_words))
        nc.gpsimd.dma_start(out=w1_raw[:], in_=words_of(w1_words))
        load_scale_rows(nc.sync, w1s_raw, w1_scales, range(4))
        nc.scalar.activation(out=warm_out[:], in_=warm_in[:], func=ACT.Sigmoid)
        nc.sync.dma_start(n1_sb[:], n1)
        nc.sync.dma_start(n2_sb[:], n2)
        nc.sync.dma_start(n3_sb[:], n3)
        nc.sync.dma_start(n4_sb[:], n4)
        nc.sync.dma_start(out=gain[:], in_=gn.rearrange("(p t) o -> p (t o)", t=PACK))
        load_scale_rows(nc.gpsimd, w2s_raw, w2_scales, range(1))
        nc.gpsimd.dma_start(out=w2_raw[:], in_=words_of(w2_words))
        load_scale_rows(nc.gpsimd, w2s_raw, w2_scales, range(1, 4))

        nc.vector.tensor_copy(out=xs_got[:], in_=xs_tab[:].indirect(offs_sb[:]))
        for q in range(4):
            nc.scalar.dma_start(
                out=xs_pick[32 * q : 32 * q + 4, :].bitcast(I32), in_=xs_got[32 * q : 32 * q + 32 : 8, :].bitcast(I32)
            )

        w1_sc = keep.tile([P, H], U8, name="w1_sc", tag="xs_then_w1s", align_bytes=64)
        deal_scales(nc, w1_sc, w1s_raw)

        x_pick = keep.tile([P, S], I32, name="x_pick", align_bytes=64)
        halves = [slice(0, HALF), slice(HALF, S)]
        quarters = [slice(c * P, (c + 1) * P) for c in range(4)]
        for c in range(2):
            nc.vector.tensor_copy(
                out=x_pick[:, halves[c]].bitcast(U32),
                in_=x_tab[:].bitcast(U32).indirect(offs_sb[:, c * HALF // 16 : (c + 1) * HALF // 16]),
            )

        w1_codes = keep.tile([P, H], I32, name="w1_codes", tag="x_then_w1", align_bytes=64)
        deal_words(nc, w1_codes, w1_raw, slice(0, 1))
        deal_words(nc, w1_codes, w1_raw, slice(1, PACK))
        w2_codes = keep.tile([P, N], I32, name="w2_codes", tag="w1_then_w2", align_bytes=64)

        def rows_out(name, w_codes, w_scales, codes, scales, order, pieces):
            tiles, banks = {}, {}
            for n, t in enumerate(order):
                tile = keep.tile([P, S], F32, name="%s%d" % (name, t), align_bytes=64)
                for c, cols in enumerate(pieces if n == 0 else [slice(0, S)]):
                    tag = "piece%d" % c if n == 0 else "bank%d" % n
                    bank = psum.tile([P, cols.stop - cols.start], F32, name="%s_%s" % (name, tag), tag=tag)
                    product(nc, bank[:], w_codes, w_scales, t, codes[:, cols], scales[:, cols])
                    nc.scalar.copy(out=tile[:, cols], in_=bank[:])
                    banks[t, cols.start] = bank
                tiles[t] = tile
            return tiles, banks

        deal_words(nc, w2_codes, w2_raw, slice(0, PACK))
        y, y_banks = rows_out("y", w1_codes, w1_sc, x_pick, xs_pick, PLANE_ORDER, [halves[0]] + quarters[2:])

        z_bf = keep.tile([P, S, PACK], BF16, name="z_bf", align_bytes=64)
        a = keep.tile([P, PACK, W], F32, name="a")
        na = keep.tile([P, PACK, W], F32, name="na")
        v, rv, dt = {}, {}, {}

        def fetch_a(n):
            nc.vector.tensor_scalar(
                out=a[:, n, :],
                in0=y[PLANE_ORDER[n]][:].indirect(n1_sb[:]),
                scalar1=0.5,
                scalar2=0.0,
                op0=ALU.mult,
                op1=ALU.add,
            )
            if n % 2 == 1:
                nc.scalar.activation(out=na[:, n - 1 : n + 1, :], in_=a[:, n - 1 : n + 1, :], func=ACT.Copy, scale=-1.0)

        def fetch_v(n):
            v[n] = ring.tile([P, W], F32, name="v")
            nc.vector.tensor_tensor(
                out=v[n][:], in0=y[PLANE_ORDER[n]][:].indirect(n2_sb[:]), in1=na[:, n, :], op=ALU.add
            )

        def positive_part(n):
            rv[n] = ring.tile([P, W], F32, name="rv")
            nc.scalar.activation(out=rv[n][:], in_=v[n][:], func=ACT.Relu)

        def put_ra(n):
            t = PLANE_ORDER[n]
            dt[t] = keep.tile([P, S], F32, name="dt%d" % t, align_bytes=64)
            nc.vector.tensor_tensor(out=dt[t][:].indirect(n1_sb[:]), in0=v[n][:], in1=na[:, n, :], op=ALU.add)

        def put_rb(n):
            t = PLANE_ORDER[n]
            nc.vector.tensor_tensor(out=dt[t][:].indirect(n2_sb[:]), in0=a[:, n, :], in1=rv[n][:], op=ALU.add)

        def scale_on_scalar(t, cols):
            nc.scalar.activation(out=z_bf[:, cols, t], in_=dt[t][:, cols], func=ACT.Copy, scale=gain[:, t : t + 1])

        def scale_on_vector(t, cols):
            nc.vector.tensor_scalar(
                out=z_bf[:, cols, t], in0=dt[t][:, cols], scalar1=gain[:, t : t + 1], scalar2=None, op0=ALU.mult
            )

        for n in range(PACK):
            fetch_a(n)
        for n in range(PACK):
            fetch_v(n)
            positive_part(n)
        put_ra(0)
        for n in range(PACK - 1):
            put_ra(n + 1)
            put_rb(n)
            scale_on_scalar(PLANE_ORDER[n], slice(0, S))
        last = PLANE_ORDER[-1]
        w2_sc = keep.tile([P, N], U8, name="w2_sc", tag="dt%d" % PLANE_ORDER[0], align_bytes=64)
        deal_scales(nc, w2_sc, w2s_raw)
        put_rb(PACK - 1)
        z_codes = keep.tile([P, S], I32, name="z_codes", align_bytes=64)
        z_sc = keep.tile([P, S], U8, name="z_sc", align_bytes=64)

        def quantize_z(cols):
            nc.vector.quantize_mx(
                out=z_codes[:, cols].bitcast(FP8X4),
                scales=z_sc[:, cols],
                in_=z_bf[:, cols, :].rearrange("p j t -> p (j t)"),
            )

        scale_on_scalar(last, quarters[3])
        scale_on_vector(last, quarters[0])
        scale_on_vector(last, quarters[1])
        quantize_z(quarters[0])
        scale_on_vector(last, quarters[2])
        for cols in quarters[1:]:
            quantize_z(cols)

        h, h_banks = rows_out("h", w2_codes, w2_sc, z_codes, z_sc, range(PACK), quarters)

        o_codes = keep.tile([P, S], I32, name="o_codes", align_bytes=64)
        o_sc = keep.tile([P, S], U8, name="o_sc", align_bytes=64)
        out_rows = out_0.rearrange("(p t) j -> p t j", t=PACK)
        out_words = words_of(out_1)

        steps = []
        start = 0
        for width in CHUNKS:
            steps.extend([(start, width, t) for t in range(PACK)])
            start = start + width
        first, gate, res = {}, {}, {}

        def entries(sb, start, width):
            return sb[:, start // 16 : (start + width) // 16]

        def fetch_first(step):
            start, width, t = step
            first[step] = ring.tile([P, width], F32, name="first")
            nc.vector.tensor_copy(out=first[step][:], in_=h[t][:].indirect(entries(n3_sb, start, width)))

        def fetch_second(step):
            start, width, t = step
            diff = ring.tile([P, width], F32, name="diff")
            gate[step] = ring.tile([P, width], F32, name="gate")
            looked_up = h[t][:].indirect(entries(n4_sb, start, width))
            if start + width == S:
                nc.vector.tensor_tensor(out=diff[:], in0=looked_up, in1=first[step][:], op=ALU.subtract)
            else:
                second = ring.tile([P, width], F32, name="second")
                nc.vector.tensor_copy(out=second[:], in_=looked_up)
                nc.gpsimd.tensor_tensor(out=diff[:], in0=second[:], in1=first[step][:], op=ALU.subtract)
            nc.scalar.activation(out=gate[step][:], in_=diff[:], func=ACT.Sigmoid, scale=-1.0)

        def finish(step):
            start, width, t = step
            cols = slice(start, start + width)
            if t == 0:
                res[start] = keep.tile([P, PACK, width], F32, name="res%d" % start)
            parts = [slice(0, width // 2), slice(width // 2, width)] if step == steps[-1] else [slice(0, width)]
            for part in parts:
                at = slice(start + part.start, start + part.stop)
                if t < ON_GPSIMD and start == 0:
                    nc.gpsimd.tensor_tensor(out=res[start][:, t, part], in0=h[t][:, at], in1=gate[step][:, part], op=ALU.mult)
                else:
                    nc.vector.tensor_tensor(
                        out=res[start][:, t, part], in0=h_banks[t, 0][:, at] if t > 0 else h_banks[t, start][:, part], in1=gate[step][:, part], op=ALU.mult
                    )
            if t == PACK - 1:
                nc.sync.dma_start(out=out_rows[:, :, cols], in_=res[start][:])
                o_bf = keep.tile([P, width, PACK], BF16, name="o_bf%d" % start, align_bytes=64)
                for part in parts:
                    dst = o_bf[:, part, :].rearrange("p (c i) t -> p c t i", i=4)
                    src = res[start][:, :, part].rearrange("p t (c i) -> p c t i", i=4)
                    if step == steps[-1]:
                        nc.vector.tensor_copy(out=dst, in_=src)
                    else:
                        nc.scalar.copy(out=dst, in_=src)
                for part in parts:
                    at = slice(start + part.start, start + part.stop)
                    nc.vector.quantize_mx(
                        out=o_codes[:, at].bitcast(FP8X4),
                        scales=o_sc[:, at],
                        in_=o_bf[:, part, :].rearrange("p j t -> p (j t)"),
                    )
                nc.sync.dma_start(out=out_words[:, cols], in_=o_codes[:, cols])

        ahead = len(steps) - PACK
        for n in range(len(steps) + 2):
            if n <= ahead:
                fetch_first(steps[n])
            if ahead <= n < len(steps) - 1:
                fetch_first(steps[n + 1])
            if n < len(steps):
                fetch_second(steps[n])
            if n >= 2:
                finish(steps[n - 2])

        for q in range(4):
            engine = nc.scalar if q < 3 else nc.sync
            engine.dma_start(out=out_2[0, 4 * q : 4 * q + 4, :].bitcast(I32), in_=o_sc[32 * q : 32 * q + 4, :].bitcast(I32))
